import numpy as np
import ml_dtypes


def mxq(x, axis, fmt="e4m3"):
    dtype, down = {"e4m3": (ml_dtypes.float8_e4m3fn, 7), "e5m2": (ml_dtypes.float8_e5m2, 14)}[fmt]
    v = np.moveaxis(np.asarray(x, np.float32).astype(ml_dtypes.bfloat16).astype(np.float64), axis, -1)
    blocks = v.reshape(v.shape[:-1] + (-1, 32))
    amax = np.abs(blocks).max(-1, keepdims=True)
    byte = np.maximum(np.where(amax > 0, np.frexp(amax)[1] - 1 + 127, 0) - down, 1)
    scale = np.exp2(byte - 127.0)
    codes = (blocks / scale).astype(np.float32).astype(dtype).astype(np.float64)
    return np.moveaxis((codes * scale).reshape(v.shape), -1, axis)


WIDE = False


def mx_kscale(k):
    if not WIDE:
        return np.ones(k)
    levels = np.array([10, -10, 5, -5, 0])
    if k % 512:
        return np.exp2(np.random.permutation(np.resize(levels, k // 32))).repeat(32)
    a = np.empty((k // 512, 16))
    for p in range(k // 512):
        a[p, :8] = np.random.permutation(np.resize(levels, 8))
        for g in range(8):
            far = levels[np.abs(levels - a[p, g]) >= 10]
            a[p, g + 8] = far[np.random.randint(len(far))]
    return np.exp2(a.ravel()).repeat(32)


def f64(x):
    return np.asarray(x).astype(np.float64)


def striped(idx):
    return np.tile(np.asarray(idx).reshape(-1, 16).T, (8, 1)).astype(np.uint16)


def unstriped(offs):
    return offs[:16].T.reshape(-1).astype(np.int64)


E2M1 = np.array([0.0, 0.5, 1.0, 1.5, 2.0, 3.0, 4.0, 6.0, -0.0, -0.5, -1.0, -1.5, -2.0, -3.0, -4.0, -6.0])


def pack_weight(w, fmt):
    k, n = w.shape
    w = f64(np.asarray(w, np.float32).astype(ml_dtypes.bfloat16)).reshape(k // 32, 32, n)
    amax = np.abs(w).max(1)
    if fmt == "e4m3":
        byte = np.frexp(amax)[1] - 1 + 127 - 7
    else:
        mant, ex = np.frexp(amax / 6.0)
        byte = np.where(mant > 0.5, ex, ex - 1) + 127
    byte = np.clip(np.where(amax > 0, byte, 1), 1, 254)
    scaled = (w * np.exp2(127.0 - byte)[:, None, :]).reshape(k, n).astype(np.float32)
    by_word = np.ascontiguousarray(scaled.reshape(k // 512, 128, 4, n).transpose(0, 1, 3, 2))
    if fmt == "e4m3":
        words = by_word.astype(ml_dtypes.float8_e4m3fn).view(np.uint8)
    else:
        c = by_word.astype(ml_dtypes.float4_e2m1fn).view(np.uint8) & 0xF
        words = (c[..., 0::2] | (c[..., 1::2] << 4)).reshape(k // 512, 128, 2 * n)
    return np.ascontiguousarray(words), np.ascontiguousarray(byte.astype(np.uint8).reshape(k // 512, 16, n))


def unpack_weight(words, scales, fmt):
    g, _, n = scales.shape
    words = np.ascontiguousarray(words).reshape(g, 128, n, -1)
    if fmt == "e4m3":
        vals = words.view(ml_dtypes.float8_e4m3fn).astype(np.float64)
    else:
        nib = np.empty((g, 128, n, 4), np.uint8)
        nib[..., 0::2] = words & 0xF
        nib[..., 1::2] = words >> 4
        vals = E2M1[nib]
    vals = vals * np.repeat(np.exp2(scales.astype(np.float64) - 127.0), 8, axis=1)[..., None]
    return vals.transpose(0, 1, 3, 2).reshape(g * 512, n)


B, N, T, D, DV, NQ = 1, 512, 2048, 512, 0, 256
PAGE = 32
SEG = 32


def setup_inputs():
    n = np.random.standard_normal
    pages = np.random.permutation(T // PAGE)[:B * N // PAGE]
    idx = (pages[:, None] * PAGE + np.arange(PAGE)[None, :]).reshape(-1)
    s = mx_kscale(D)[:, None]
    kp = pack_weight(n((D, T)) / s, "e4m3")
    return {
        "qT": (n((B, D, NQ)) * s * (1.00 / np.sqrt(D))).astype(np.float32),
        "k_words": kp[0],
        "k_scales": kp[1],
        "offs": striped(idx),
    }


def reference(qT, k_words, k_scales, offs):
    idx = unstriped(offs)
    pool = unpack_weight(k_words, k_scales, "e4m3")
    pick = lambda x: x[:, idx].reshape(x.shape[0], B, N).transpose(1, 0, 2)
    a = mxq(f64(qT), 1, "e4m3").transpose(0, 2, 1) @ pick(pool)
    return a.reshape(B, NQ, N // SEG, SEG).max(-1)

@@ -1,0 +1,79 @@
+from contextlib import ExitStack
+
+import concourse.mybir as mybir
+
+N, T, DIM, NQ, SEG = 512, 2048, 512, 256, 32
+
+F32 = mybir.dt.float32
+BF16 = mybir.dt.bfloat16
+I32 = mybir.dt.int32
+U32 = mybir.dt.uint32
+U16 = mybir.dt.uint16
+U8 = mybir.dt.uint8
+FP8X4 = mybir.dt.float8_e4m3fn_x4
+
+P = 128
+PACK = 4
+HALF = N // 2
+FLOPS = 2 * NQ * N * DIM
+
+
+def tile_attend_maxsim_kernel(tc, qT, k_words, k_scales, offs, out):
+    nc = tc.nc
+    with ExitStack() as ctx:
+        keep = ctx.enter_context(tc.tile_pool(name="keep", bufs=1))
+        psum = ctx.enter_context(tc.psum_pool(name="psum", bufs=1))
+
+        offsets = keep.tile([P, N // 16], U16, name="offsets")
+        pool_scales = keep.tile([P, T // 4], I32, name="pool_scales", align_bytes=64)
+        pool_words = keep.tile([P, T], I32, name="pool_words", align_bytes=64)
+        q_raw = keep.tile([P, PACK, NQ], F32, name="q_raw", align_bytes=64)
+
+        nc.vector.memset(pool_scales[:], 0)
+        nc.sync.dma_start(offsets[:], offs)
+        nc.sync.dma_start(out=q_raw[:], in_=qT[0].rearrange("(p j) w -> p j w", j=PACK))
+        scale_rows = k_scales[0].bitcast(I32)
+        for f in range(4):
+            nc.sync.dma_start(out=pool_scales[f:P:32, :], in_=scale_rows[f:16:4, :])
+        nc.sync.dma_start(out=pool_words[:], in_=k_words[0].rearrange("p t r -> p (t r)").bitcast(I32))
+
+        q_bf = keep.tile([P, NQ, PACK], BF16, name="q_bf", align_bytes=64)
+        nc.vector.tensor_copy(out=q_bf[:], in_=q_raw[:].rearrange("p j w -> p w j"))
+        key_scales = keep.tile([P, N], U8, name="key_scales", align_bytes=64)
+        nc.vector.tensor_copy(key_scales[:], pool_scales[:].bitcast(U8).indirect(offsets[:]))
+        q_codes = keep.tile([P, NQ], U32, name="q_codes", align_bytes=64)
+        q_scales = keep.tile([P, NQ], U8, name="q_scales", align_bytes=64)
+        nc.vector.quantize_mx(
+            out=q_codes[:].bitcast(FP8X4),
+            scales=q_scales[:],
+            in_=q_bf[:].rearrange("p w j -> p (w j)"),
+        )
+
+        key_words = []
+        for c in range(2):
+            kw = keep.tile([P, HALF], U32, name="key_words%d" % c, align_bytes=64)
+            cols = slice(c * HALF // 16, (c + 1) * HALF // 16)
+            nc.vector.tensor_copy(kw[:], pool_words[:].bitcast(U32).indirect(offsets[:, cols]))
+            key_words.append(kw)
+
+        best = [keep.tile([P, N // SEG], F32, name="best%d" % h, align_bytes=64) for h in range(2)]
+        for c in range(2):
+            for h in range(2):
+                scores = psum.tile([P, HALF], F32, name="scores%d%d" % (c, h))
+                nc.tensor.matmul_mx(
+                    out=scores[:],
+                    lhsT=q_codes[:, h * P : (h + 1) * P].bitcast(FP8X4),
+                    lhsT_scale=q_scales[:, h * P : (h + 1) * P],
+                    rhs=key_words[c][:].bitcast(FP8X4),
+                    rhs_scale=key_scales[:, c * HALF : (c + 1) * HALF],
+                    start=True,
+                    stop=True,
+                )
+                nc.vector.tensor_reduce(
+                    out=best[h][:, c * 8 : (c + 1) * 8],
+                    in_=scores[:].rearrange("p (j s) -> p j s", s=SEG),
+                    axis=mybir.AxisListType.X,
+                    op=mybir.AluOpType.max,
+                )
+                if c == 1:
+                    nc.sync.dma_start(out=out[0, h * P : (h + 1) * P, :], in_=best[h][:])

@@ -30,8 +30,8 @@ def tile_attend_maxsim_kernel(tc, qT, k_words, k_scales, offs, out):
         q_raw = keep.tile([P, PACK, NQ], F32, name="q_raw", align_bytes=64)
 
         nc.vector.memset(pool_scales[:], 0)
-        nc.sync.dma_start(offsets[:], offs)
         nc.sync.dma_start(out=q_raw[:], in_=qT[0].rearrange("(p j) w -> p j w", j=PACK))
+        nc.sync.dma_start(offsets[:], offs)
         scale_rows = k_scales[0].bitcast(I32)
         for f in range(4):
             nc.sync.dma_start(out=pool_scales[f:P:32, :], in_=scale_rows[f:16:4, :])
@@ -39,8 +39,6 @@ def tile_attend_maxsim_kernel(tc, qT, k_words, k_scales, offs, out):
 
         q_bf = keep.tile([P, NQ, PACK], BF16, name="q_bf", align_bytes=64)
         nc.vector.tensor_copy(out=q_bf[:], in_=q_raw[:].rearrange("p j w -> p w j"))
-        key_scales = keep.tile([P, N], U8, name="key_scales", align_bytes=64)
-        nc.vector.tensor_copy(key_scales[:], pool_scales[:].bitcast(U8).indirect(offsets[:]))
         q_codes = keep.tile([P, NQ], U32, name="q_codes", align_bytes=64)
         q_scales = keep.tile([P, NQ], U8, name="q_scales", align_bytes=64)
         nc.vector.quantize_mx(
@@ -49,6 +47,8 @@ def tile_attend_maxsim_kernel(tc, qT, k_words, k_scales, offs, out):
             in_=q_bf[:].rearrange("p w j -> p (w j)"),
         )
 
+        key_scales = keep.tile([P, N], U8, name="key_scales", align_bytes=64)
+        nc.vector.tensor_copy(key_scales[:], pool_scales[:].bitcast(U8).indirect(offsets[:]))
         key_words = []
         for c in range(2):
             kw = keep.tile([P, HALF], U32, name="key_words%d" % c, align_bytes=64)

@@ -37,18 +37,23 @@ def tile_attend_maxsim_kernel(tc, qT, k_words, k_scales, offs, out):
             nc.sync.dma_start(out=pool_scales[f:P:32, :], in_=scale_rows[f:16:4, :])
         nc.sync.dma_start(out=pool_words[:], in_=k_words[0].rearrange("p t r -> p (t r)").bitcast(I32))
 
-        q_bf = keep.tile([P, NQ, PACK], BF16, name="q_bf", align_bytes=64)
-        nc.vector.tensor_copy(out=q_bf[:], in_=q_raw[:].rearrange("p j w -> p w j"))
         q_codes = keep.tile([P, NQ], U32, name="q_codes", align_bytes=64)
         q_scales = keep.tile([P, NQ], U8, name="q_scales", align_bytes=64)
-        nc.vector.quantize_mx(
-            out=q_codes[:].bitcast(FP8X4),
-            scales=q_scales[:],
-            in_=q_bf[:].rearrange("p w j -> p (w j)"),
-        )
-
+        q_bf = [keep.tile([P, P, PACK], BF16, name="q_bf%d" % h, align_bytes=64) for h in range(2)]
+        for h, cast in enumerate((nc.vector.tensor_copy, nc.scalar.copy)):
+            cast(
+                out=q_bf[h][:].rearrange("p (c i) j -> p c j i", i=4),
+                in_=q_raw[:, :, h * P : (h + 1) * P].rearrange("p j (c i) -> p c j i", i=4),
+            )
         key_scales = keep.tile([P, N], U8, name="key_scales", align_bytes=64)
         nc.vector.tensor_copy(key_scales[:], pool_scales[:].bitcast(U8).indirect(offsets[:]))
+        for h in range(2):
+            nc.vector.quantize_mx(
+                out=q_codes[:, h * P : (h + 1) * P].bitcast(FP8X4),
+                scales=q_scales[:, h * P : (h + 1) * P],
+                in_=q_bf[h][:].rearrange("p w j -> p (w j)"),
+            )
+
         key_words = []
         for c in range(2):
             kw = keep.tile([P, HALF], U32, name="key_words%d" % c, align_bytes=64)

@@ -43,7 +43,7 @@ def tile_attend_maxsim_kernel(tc, qT, k_words, k_scales, offs, out):
         for h, cast in enumerate((nc.vector.tensor_copy, nc.scalar.copy)):
             cast(
                 out=q_bf[h][:].rearrange("p (c i) j -> p c j i", i=4),
-                in_=q_raw[:, :, h * P : (h + 1) * P].rearrange("p j (c i) -> p c j i", i=4),
+                in_=q_raw[:, :, h:NQ:2].rearrange("p j (c i) -> p c j i", i=4),
             )
         key_scales = keep.tile([P, N], U8, name="key_scales", align_bytes=64)
         nc.vector.tensor_copy(key_scales[:], pool_scales[:].bitcast(U8).indirect(offsets[:]))
@@ -61,7 +61,7 @@ def tile_attend_maxsim_kernel(tc, qT, k_words, k_scales, offs, out):
             nc.vector.tensor_copy(kw[:], pool_words[:].bitcast(U32).indirect(offsets[:, cols]))
             key_words.append(kw)
 
-        best = [keep.tile([P, N // SEG], F32, name="best%d" % h, align_bytes=64) for h in range(2)]
+        best = keep.tile([P, 2, N // SEG], F32, name="best", align_bytes=64)
         for c in range(2):
             for h in range(2):
                 scores = psum.tile([P, HALF], F32, name="scores%d%d" % (c, h))
@@ -75,10 +75,9 @@ def tile_attend_maxsim_kernel(tc, qT, k_words, k_scales, offs, out):
                     stop=True,
                 )
                 nc.vector.tensor_reduce(
-                    out=best[h][:, c * 8 : (c + 1) * 8],
+                    out=best[:, h, c * 8 : (c + 1) * 8],
                     in_=scores[:].rearrange("p (j s) -> p j s", s=SEG),
                     axis=mybir.AxisListType.X,
                     op=mybir.AluOpType.max,
                 )
-                if c == 1:
-                    nc.sync.dma_start(out=out[0, h * P : (h + 1) * P, :], in_=best[h][:])
+        nc.sync.dma_start(out=out[0].rearrange("(p h) j -> p h j", h=2), in_=best[:])

@@ -1,6 +1,7 @@
 from contextlib import ExitStack
 
 import concourse.mybir as mybir
+from concourse.masks import make_identity
 
 N, T, DIM, NQ, SEG = 512, 2048, 512, 256, 32
 
@@ -36,6 +37,14 @@ def tile_attend_maxsim_kernel(tc, qT, k_words, k_scales, offs, out):
         for f in range(4):
             nc.sync.dma_start(out=pool_scales[f:P:32, :], in_=scale_rows[f:16:4, :])
         nc.sync.dma_start(out=pool_words[:], in_=k_words[0].rearrange("p t r -> p (t r)").bitcast(I32))
+
+        identity = keep.tile([P, P], F32, name="identity", align_bytes=64)
+        make_identity(nc, identity[:])
+        warm = [psum.tile([P, 4, P], F32, name="warm%d" % b) for b in range(3)]
+        for i in range(12):
+            nc.tensor.transpose(warm[i // 4][:, i % 4, :], identity[:], identity[:])
+        for i in range(12):
+            nc.tensor.transpose(warm[i // 4][:, i % 4, :], q_raw[:, i % PACK, :P], identity[:])
 
         q_codes = keep.tile([P, NQ], U32, name="q_codes", align_bytes=64)
         q_scales = keep.tile([P, NQ], U8, name="q_scales", align_bytes=64)

@@ -43,8 +43,8 @@ def tile_attend_maxsim_kernel(tc, qT, k_words, k_scales, offs, out):
         warm = [psum.tile([P, 4, P], F32, name="warm%d" % b) for b in range(3)]
         for i in range(12):
             nc.tensor.transpose(warm[i // 4][:, i % 4, :], identity[:], identity[:])
-        for i in range(12):
-            nc.tensor.transpose(warm[i // 4][:, i % 4, :], q_raw[:, i % PACK, :P], identity[:])
+        for i in range(24):
+            nc.tensor.transpose(warm[i // 4 % 3][:, i % 4, :], q_raw[:, i % PACK, :P], identity[:])
 
         q_codes = keep.tile([P, NQ], U32, name="q_codes", align_bytes=64)
         q_scales = keep.tile([P, NQ], U8, name="q_scales", align_bytes=64)

@@ -1,7 +1,6 @@
 from contextlib import ExitStack
 
 import concourse.mybir as mybir
-from concourse.masks import make_identity
 
 N, T, DIM, NQ, SEG = 512, 2048, 512, 256, 32
 
@@ -34,34 +33,27 @@ def tile_attend_maxsim_kernel(tc, qT, k_words, k_scales, offs, out):
         nc.sync.dma_start(out=q_raw[:], in_=qT[0].rearrange("(p j) w -> p j w", j=PACK))
         nc.sync.dma_start(offsets[:], offs)
         scale_rows = k_scales[0].bitcast(I32)
-        for f in range(4):
-            nc.sync.dma_start(out=pool_scales[f:P:32, :], in_=scale_rows[f:16:4, :])
+        nc.sync.dma_start(out=pool_scales[0:P:8, :], in_=scale_rows)
         nc.sync.dma_start(out=pool_words[:], in_=k_words[0].rearrange("p t r -> p (t r)").bitcast(I32))
-
-        identity = keep.tile([P, P], F32, name="identity", align_bytes=64)
-        make_identity(nc, identity[:])
-        warm = [psum.tile([P, 4, P], F32, name="warm%d" % b) for b in range(3)]
-        for i in range(12):
-            nc.tensor.transpose(warm[i // 4][:, i % 4, :], identity[:], identity[:])
-        for i in range(24):
-            nc.tensor.transpose(warm[i // 4 % 3][:, i % 4, :], q_raw[:, i % PACK, :P], identity[:])
 
         q_codes = keep.tile([P, NQ], U32, name="q_codes", align_bytes=64)
         q_scales = keep.tile([P, NQ], U8, name="q_scales", align_bytes=64)
-        q_bf = [keep.tile([P, P, PACK], BF16, name="q_bf%d" % h, align_bytes=64) for h in range(2)]
-        for h, cast in enumerate((nc.vector.tensor_copy, nc.scalar.copy)):
-            cast(
-                out=q_bf[h][:].rearrange("p (c i) j -> p c j i", i=4),
-                in_=q_raw[:, :, h:NQ:2].rearrange("p j (c i) -> p c j i", i=4),
-            )
+        q_bf = keep.tile([P, 2, P, PACK], BF16, name="q_bf", align_bytes=64)
+        nc.scalar.copy(
+            out=q_bf[:].rearrange("p h (c i) j -> p c j i h", i=2),
+            in_=q_raw[:].rearrange("p j (c i h) -> p c j i h", i=2, h=2),
+        )
+        picked = keep.tile([P, N], U8, name="picked", align_bytes=64)
         key_scales = keep.tile([P, N], U8, name="key_scales", align_bytes=64)
-        nc.vector.tensor_copy(key_scales[:], pool_scales[:].bitcast(U8).indirect(offsets[:]))
-        for h in range(2):
-            nc.vector.quantize_mx(
-                out=q_codes[:, h * P : (h + 1) * P].bitcast(FP8X4),
-                scales=q_scales[:, h * P : (h + 1) * P],
-                in_=q_bf[h][:].rearrange("p w j -> p (w j)"),
-            )
+        nc.vector.tensor_copy(picked[:], pool_scales[:].bitcast(U8).indirect(offsets[:]))
+        nc.vector.tensor_copy(key_scales[:].bitcast(I32), picked[:].bitcast(I32))
+        for r, queue in ((1, nc.sync), (2, nc.scalar), (3, nc.sync)):
+            queue.dma_start(out=key_scales[r:P:32, :].bitcast(I32), in_=picked[8 * r : P : 32, :].bitcast(I32))
+        nc.vector.quantize_mx(
+            out=q_codes[:].bitcast(FP8X4),
+            scales=q_scales[:],
+            in_=q_bf[:].rearrange("p h w j -> p (h w j)"),
+        )
 
         key_words = []
         for c in range(2):

@@ -25,7 +25,7 @@ def tile_attend_maxsim_kernel(tc, qT, k_words, k_scales, offs, out):
         psum = ctx.enter_context(tc.psum_pool(name="psum", bufs=1))
 
         offsets = keep.tile([P, N // 16], U16, name="offsets")
-        pool_scales = keep.tile([P, T // 4], I32, name="pool_scales", align_bytes=64)
+        pool_scales = keep.tile([P, T // 4], I32, name="pool_scales", tag="scales_then_q", align_bytes=64)
         pool_words = keep.tile([P, T], I32, name="pool_words", align_bytes=64)
         q_raw = keep.tile([P, PACK, NQ], F32, name="q_raw", align_bytes=64)
 
@@ -38,22 +38,27 @@ def tile_attend_maxsim_kernel(tc, qT, k_words, k_scales, offs, out):
 
         q_codes = keep.tile([P, NQ], U32, name="q_codes", align_bytes=64)
         q_scales = keep.tile([P, NQ], U8, name="q_scales", align_bytes=64)
-        q_bf = keep.tile([P, 2, P, PACK], BF16, name="q_bf", align_bytes=64)
-        nc.scalar.copy(
-            out=q_bf[:].rearrange("p h (c i) j -> p c j i h", i=2),
-            in_=q_raw[:].rearrange("p j (c i h) -> p c j i h", i=2, h=2),
-        )
         picked = keep.tile([P, N], U8, name="picked", align_bytes=64)
         key_scales = keep.tile([P, N], U8, name="key_scales", align_bytes=64)
         nc.vector.tensor_copy(picked[:], pool_scales[:].bitcast(U8).indirect(offsets[:]))
         nc.vector.tensor_copy(key_scales[:].bitcast(I32), picked[:].bitcast(I32))
         for r, queue in ((1, nc.sync), (2, nc.scalar), (3, nc.sync)):
             queue.dma_start(out=key_scales[r:P:32, :].bitcast(I32), in_=picked[8 * r : P : 32, :].bitcast(I32))
-        nc.vector.quantize_mx(
-            out=q_codes[:].bitcast(FP8X4),
-            scales=q_scales[:],
-            in_=q_bf[:].rearrange("p h w j -> p (h w j)"),
-        )
+        q_bf = [
+            keep.tile([P, P, PACK], BF16, name="q_bf0", tag="scales_then_q", align_bytes=64),
+            keep.tile([P, P, PACK], BF16, name="q_bf1", align_bytes=64),
+        ]
+        for h, cast in enumerate((nc.vector.tensor_copy, nc.scalar.copy)):
+            cast(
+                out=q_bf[h][:].rearrange("p (c i) j -> p c j i", i=4),
+                in_=q_raw[:, :, h:NQ:2].rearrange("p j (c i) -> p c j i", i=4),
+            )
+        for h in (1, 0):
+            nc.vector.quantize_mx(
+                out=q_codes[:, h * P : (h + 1) * P].bitcast(FP8X4),
+                scales=q_scales[:, h * P : (h + 1) * P],
+                in_=q_bf[h][:].rearrange("p w j -> p (w j)"),
+            )
 
         key_words = []
         for c in range(2):

@@ -29,21 +29,24 @@ def tile_attend_maxsim_kernel(tc, qT, k_words, k_scales, offs, out):
         pool_words = keep.tile([P, T], I32, name="pool_words", align_bytes=64)
         q_raw = keep.tile([P, PACK, NQ], F32, name="q_raw", align_bytes=64)
 
+        key_scales = keep.tile([P, N // 4], I32, name="key_scales", align_bytes=64)
         nc.vector.memset(pool_scales[:], 0)
+        nc.vector.memset(key_scales[:], 0)
         nc.sync.dma_start(out=q_raw[:], in_=qT[0].rearrange("(p j) w -> p j w", j=PACK))
         nc.sync.dma_start(offsets[:], offs)
         scale_rows = k_scales[0].bitcast(I32)
-        nc.sync.dma_start(out=pool_scales[0:P:8, :], in_=scale_rows)
+        nc.sync.dma_start(out=pool_scales[0:16, :], in_=scale_rows)
         nc.sync.dma_start(out=pool_words[:], in_=k_words[0].rearrange("p t r -> p (t r)").bitcast(I32))
 
         q_codes = keep.tile([P, NQ], U32, name="q_codes", align_bytes=64)
         q_scales = keep.tile([P, NQ], U8, name="q_scales", align_bytes=64)
         picked = keep.tile([P, N], U8, name="picked", align_bytes=64)
-        key_scales = keep.tile([P, N], U8, name="key_scales", align_bytes=64)
         nc.vector.tensor_copy(picked[:], pool_scales[:].bitcast(U8).indirect(offsets[:]))
-        nc.vector.tensor_copy(key_scales[:].bitcast(I32), picked[:].bitcast(I32))
-        for r, queue in ((1, nc.sync), (2, nc.scalar), (3, nc.sync)):
-            queue.dma_start(out=key_scales[r:P:32, :].bitcast(I32), in_=picked[8 * r : P : 32, :].bitcast(I32))
+        for quad, queue in ((1, nc.sync), (2, nc.scalar), (3, nc.sync)):
+            queue.dma_start(
+                out=key_scales[32 * quad : 32 * quad + 4, :], in_=picked[4 * quad : 4 * quad + 4, :].bitcast(I32)
+            )
+        nc.vector.tensor_copy(key_scales[0:4, :], picked[0:4, :].bitcast(I32))
         q_bf = [
             keep.tile([P, P, PACK], BF16, name="q_bf0", tag="scales_then_q", align_bytes=64),
             keep.tile([P, P, PACK], BF16, name="q_bf1", align_bytes=64),
@@ -76,7 +79,7 @@ def tile_attend_maxsim_kernel(tc, qT, k_words, k_scales, offs, out):
                     lhsT=q_codes[:, h * P : (h + 1) * P].bitcast(FP8X4),
                     lhsT_scale=q_scales[:, h * P : (h + 1) * P],
                     rhs=key_words[c][:].bitcast(FP8X4),
-                    rhs_scale=key_scales[:, c * HALF : (c + 1) * HALF],
+                    rhs_scale=key_scales[:].bitcast(U8)[:, c * HALF : (c + 1) * HALF],
                     start=True,
                     stop=True,
                 )

@@ -25,11 +25,11 @@ def tile_attend_maxsim_kernel(tc, qT, k_words, k_scales, offs, out):
         psum = ctx.enter_context(tc.psum_pool(name="psum", bufs=1))
 
         offsets = keep.tile([P, N // 16], U16, name="offsets")
-        pool_scales = keep.tile([P, T // 4], I32, name="pool_scales", tag="scales_then_q", align_bytes=64)
-        pool_words = keep.tile([P, T], I32, name="pool_words", align_bytes=64)
-        q_raw = keep.tile([P, PACK, NQ], F32, name="q_raw", align_bytes=64)
+        pool_scales = keep.tile([P, T // 4], I32, name="pool_scales", tag="scales_then_q", align_bytes=256)
+        pool_words = keep.tile([P, T], I32, name="pool_words", align_bytes=256)
+        q_raw = keep.tile([P, PACK, NQ], F32, name="q_raw", align_bytes=256)
 
-        key_scales = keep.tile([P, N // 4], I32, name="key_scales", align_bytes=64)
+        key_scales = keep.tile([P, N // 4], I32, name="key_scales", align_bytes=256)
         nc.vector.memset(pool_scales[:], 0)
         nc.vector.memset(key_scales[:], 0)
         nc.sync.dma_start(out=q_raw[:], in_=qT[0].rearrange("(p j) w -> p j w", j=PACK))
@@ -38,9 +38,9 @@ def tile_attend_maxsim_kernel(tc, qT, k_words, k_scales, offs, out):
         nc.sync.dma_start(out=pool_scales[0:16, :], in_=scale_rows)
         nc.sync.dma_start(out=pool_words[:], in_=k_words[0].rearrange("p t r -> p (t r)").bitcast(I32))
 
-        q_codes = keep.tile([P, NQ], U32, name="q_codes", align_bytes=64)
-        q_scales = keep.tile([P, NQ], U8, name="q_scales", align_bytes=64)
-        picked = keep.tile([P, N], U8, name="picked", align_bytes=64)
+        q_codes = keep.tile([P, NQ], U32, name="q_codes", align_bytes=256)
+        q_scales = keep.tile([P, NQ], U8, name="q_scales", align_bytes=256)
+        picked = keep.tile([P, N], U8, name="picked", align_bytes=256)
         nc.vector.tensor_copy(picked[:], pool_scales[:].bitcast(U8).indirect(offsets[:]))
         for quad, queue in ((1, nc.sync), (2, nc.scalar), (3, nc.sync)):
             queue.dma_start(
@@ -48,8 +48,8 @@ def tile_attend_maxsim_kernel(tc, qT, k_words, k_scales, offs, out):
             )
         nc.vector.tensor_copy(key_scales[0:4, :], picked[0:4, :].bitcast(I32))
         q_bf = [
-            keep.tile([P, P, PACK], BF16, name="q_bf0", tag="scales_then_q", align_bytes=64),
-            keep.tile([P, P, PACK], BF16, name="q_bf1", align_bytes=64),
+            keep.tile([P, P, PACK], BF16, name="q_bf0", tag="scales_then_q", align_bytes=256),
+            keep.tile([P, P, PACK], BF16, name="q_bf1", align_bytes=256),
         ]
         for h, cast in enumerate((nc.vector.tensor_copy, nc.scalar.copy)):
             cast(
@@ -65,12 +65,12 @@ def tile_attend_maxsim_kernel(tc, qT, k_words, k_scales, offs, out):
 
         key_words = []
         for c in range(2):
-            kw = keep.tile([P, HALF], U32, name="key_words%d" % c, align_bytes=64)
+            kw = keep.tile([P, HALF], U32, name="key_words%d" % c, align_bytes=256)
             cols = slice(c * HALF // 16, (c + 1) * HALF // 16)
             nc.vector.tensor_copy(kw[:], pool_words[:].bitcast(U32).indirect(offsets[:, cols]))
             key_words.append(kw)
 
-        best = keep.tile([P, 2, N // SEG], F32, name="best", align_bytes=64)
+        best = keep.tile([P, 2, N // SEG], F32, name="best", align_bytes=256)
         for c in range(2):
             for h in range(2):
                 scores = psum.tile([P, HALF], F32, name="scores%d%d" % (c, h))

@@ -71,22 +71,22 @@ def tile_attend_maxsim_kernel(tc, qT, k_words, k_scales, offs, out):
             key_words.append(kw)
 
         best = keep.tile([P, 2, N // SEG], F32, name="best", align_bytes=256)
-        for c in range(2):
-            for h in range(2):
-                scores = psum.tile([P, HALF], F32, name="scores%d%d" % (c, h))
-                nc.tensor.matmul_mx(
-                    out=scores[:],
-                    lhsT=q_codes[:, h * P : (h + 1) * P].bitcast(FP8X4),
-                    lhsT_scale=q_scales[:, h * P : (h + 1) * P],
-                    rhs=key_words[c][:].bitcast(FP8X4),
-                    rhs_scale=key_scales[:].bitcast(U8)[:, c * HALF : (c + 1) * HALF],
-                    start=True,
-                    stop=True,
-                )
-                nc.vector.tensor_reduce(
-                    out=best[:, h, c * 8 : (c + 1) * 8],
-                    in_=scores[:].rearrange("p (j s) -> p j s", s=SEG),
-                    axis=mybir.AxisListType.X,
-                    op=mybir.AluOpType.max,
-                )
+        for i, (h, lo, width) in enumerate([(h, c * HALF + lo, P) for c, h in ((0, 0), (0, 1), (1, 1), (1, 0)) for lo in (0, P)]):
+            c, at = divmod(lo, HALF)
+            scores = psum.tile([P, width], F32, name="scores%d" % i)
+            nc.tensor.matmul_mx(
+                out=scores[:],
+                lhsT=q_codes[:, h * P : (h + 1) * P].bitcast(FP8X4),
+                lhsT_scale=q_scales[:, h * P : (h + 1) * P],
+                rhs=key_words[c][:, at : at + width].bitcast(FP8X4),
+                rhs_scale=key_scales[:].bitcast(U8)[:, lo : lo + width],
+                start=True,
+                stop=True,
+            )
+            nc.vector.tensor_reduce(
+                out=best[:, h, lo // SEG : (lo + width) // SEG],
+                in_=scores[:].rearrange("p (j s) -> p j s", s=SEG),
+                axis=mybir.AxisListType.X,
+                op=mybir.AluOpType.max,
+            )
         nc.sync.dma_start(out=out[0].rearrange("(p h) j -> p h j", h=2), in_=best[:])

@@ -53,8 +53,8 @@ def tile_attend_maxsim_kernel(tc, qT, k_words, k_scales, offs, out):
         ]
         for h, cast in enumerate((nc.vector.tensor_copy, nc.scalar.copy)):
             cast(
-                out=q_bf[h][:].rearrange("p (c i) j -> p c j i", i=4),
-                in_=q_raw[:, :, h:NQ:2].rearrange("p j (c i) -> p c j i", i=4),
+                out=q_bf[h][:].rearrange("p (u i b) j -> p u b j i", u=2, i=4),
+                in_=q_raw[:, :, h:NQ:2].rearrange("p j (b u i) -> p u b j i", u=2, i=4),
             )
         for h in (1, 0):
             nc.vector.quantize_mx(
@@ -89,4 +89,6 @@ def tile_attend_maxsim_kernel(tc, qT, k_words, k_scales, offs, out):
                 axis=mybir.AxisListType.X,
                 op=mybir.AluOpType.max,
             )
-        nc.sync.dma_start(out=out[0].rearrange("(p h) j -> p h j", h=2), in_=best[:])
+        nc.sync.dma_start(
+            out=out[0].rearrange("(b a h) j -> a b (h j)", a=8, h=2), in_=best[:].rearrange("p h j -> p (h j)")
+        )

@@ -14,7 +14,6 @@ FP8X4 = mybir.dt.float8_e4m3fn_x4
 
 P = 128
 PACK = 4
-HALF = N // 2
 FLOPS = 2 * NQ * N * DIM
 
 
@@ -64,15 +63,15 @@ def tile_attend_maxsim_kernel(tc, qT, k_words, k_scales, offs, out):
             )
 
         key_words = []
-        for c in range(2):
-            kw = keep.tile([P, HALF], U32, name="key_words%d" % c, align_bytes=256)
-            cols = slice(c * HALF // 16, (c + 1) * HALF // 16)
+        for c in range(N // P):
+            kw = keep.tile([P, P], U32, name="key_words%d" % c, align_bytes=256)
+            cols = slice(c * P // 16, (c + 1) * P // 16)
             nc.vector.tensor_copy(kw[:], pool_words[:].bitcast(U32).indirect(offsets[:, cols]))
             key_words.append(kw)
 
         best = keep.tile([P, 2, N // SEG], F32, name="best", align_bytes=256)
-        for i, (h, lo, width) in enumerate([(h, c * HALF + lo, P) for c, h in ((0, 0), (0, 1), (1, 1), (1, 0)) for lo in (0, P)]):
-            c, at = divmod(lo, HALF)
+        for i, (h, lo, width) in enumerate([(h, c * P, P) for c in range(N // P) for h in (1, 0)]):
+            c, at = divmod(lo, P)
             scores = psum.tile([P, width], F32, name="scores%d" % i)
             nc.tensor.matmul_mx(
                 out=scores[:],

@@ -24,21 +24,22 @@ def tile_attend_maxsim_kernel(tc, qT, k_words, k_scales, offs, out):
         psum = ctx.enter_context(tc.psum_pool(name="psum", bufs=1))
 
         offsets = keep.tile([P, N // 16], U16, name="offsets")
-        pool_scales = keep.tile([P, T // 4], I32, name="pool_scales", tag="scales_then_q", align_bytes=256)
+        pool_scales = keep.tile([P, T // 4], I32, name="pool_scales", align_bytes=256)
         pool_words = keep.tile([P, T], I32, name="pool_words", align_bytes=256)
         q_raw = keep.tile([P, PACK, NQ], F32, name="q_raw", align_bytes=256)
 
         key_scales = keep.tile([P, N // 4], I32, name="key_scales", align_bytes=256)
+        landed = keep.tile([16, T // 4], I32, name="landed", align_bytes=256)
+        nc.scalar.dma_start(out=landed[:], in_=k_scales[0].bitcast(I32))
         nc.vector.memset(pool_scales[:], 0)
         nc.vector.memset(key_scales[:], 0)
-        nc.sync.dma_start(out=q_raw[:], in_=qT[0].rearrange("(p j) w -> p j w", j=PACK))
         nc.sync.dma_start(offsets[:], offs)
-        scale_rows = k_scales[0].bitcast(I32)
-        nc.sync.dma_start(out=pool_scales[0:16, :], in_=scale_rows)
+        nc.sync.dma_start(out=q_raw[:], in_=qT[0].rearrange("(p j) w -> p j w", j=PACK))
         nc.sync.dma_start(out=pool_words[:], in_=k_words[0].rearrange("p t r -> p (t r)").bitcast(I32))
 
         q_codes = keep.tile([P, NQ], U32, name="q_codes", align_bytes=256)
         q_scales = keep.tile([P, NQ], U8, name="q_scales", align_bytes=256)
+        nc.vector.tensor_copy(pool_scales[0:16, :], landed[:])
         picked = keep.tile([P, N], U8, name="picked", align_bytes=256)
         nc.vector.tensor_copy(picked[:], pool_scales[:].bitcast(U8).indirect(offsets[:]))
         for quad, queue in ((1, nc.sync), (2, nc.scalar), (3, nc.sync)):
@@ -47,10 +48,10 @@ def tile_attend_maxsim_kernel(tc, qT, k_words, k_scales, offs, out):
             )
         nc.vector.tensor_copy(key_scales[0:4, :], picked[0:4, :].bitcast(I32))
         q_bf = [
-            keep.tile([P, P, PACK], BF16, name="q_bf0", tag="scales_then_q", align_bytes=256),
+            keep.tile([P, P, PACK], BF16, name="q_bf0", align_bytes=256),
             keep.tile([P, P, PACK], BF16, name="q_bf1", align_bytes=256),
         ]
-        for h, cast in enumerate((nc.vector.tensor_copy, nc.scalar.copy)):
+        for h, cast in enumerate((nc.vector.tensor_copy, nc.vector.tensor_copy)):
             cast(
                 out=q_bf[h][:].rearrange("p (u i b) j -> p u b j i", u=2, i=4),
                 in_=q_raw[:, :, h:NQ:2].rearrange("p j (b u i) -> p u b j i", u=2, i=4),

@@ -42,7 +42,7 @@ def tile_attend_maxsim_kernel(tc, qT, k_words, k_scales, offs, out):
         nc.vector.tensor_copy(pool_scales[0:16, :], landed[:])
         picked = keep.tile([P, N], U8, name="picked", align_bytes=256)
         nc.vector.tensor_copy(picked[:], pool_scales[:].bitcast(U8).indirect(offsets[:]))
-        for quad, queue in ((1, nc.sync), (2, nc.scalar), (3, nc.sync)):
+        for quad, queue in ((1, nc.scalar), (2, nc.sync), (3, nc.scalar)):
             queue.dma_start(
                 out=key_scales[32 * quad : 32 * quad + 4, :], in_=picked[4 * quad : 4 * quad + 4, :].bitcast(I32)
             )

@@ -29,8 +29,8 @@ def tile_attend_maxsim_kernel(tc, qT, k_words, k_scales, offs, out):
         q_raw = keep.tile([P, PACK, NQ], F32, name="q_raw", align_bytes=256)
 
         key_scales = keep.tile([P, N // 4], I32, name="key_scales", align_bytes=256)
-        landed = keep.tile([16, T // 4], I32, name="landed", align_bytes=256)
-        nc.scalar.dma_start(out=landed[:], in_=k_scales[0].bitcast(I32))
+        landed = keep.tile([P, T // 4], I32, name="landed", align_bytes=256)
+        nc.scalar.dma_start(out=landed[64:80, :], in_=k_scales[0].bitcast(I32))
         nc.vector.memset(pool_scales[:], 0)
         nc.vector.memset(key_scales[:], 0)
         nc.sync.dma_start(offsets[:], offs)
@@ -39,14 +39,15 @@ def tile_attend_maxsim_kernel(tc, qT, k_words, k_scales, offs, out):
 
         q_codes = keep.tile([P, NQ], U32, name="q_codes", align_bytes=256)
         q_scales = keep.tile([P, NQ], U8, name="q_scales", align_bytes=256)
-        nc.vector.tensor_copy(pool_scales[0:16, :], landed[:])
+        nc.vector.tensor_copy(pool_scales[64:80, :], landed[64:80, :])
         picked = keep.tile([P, N], U8, name="picked", align_bytes=256)
         nc.vector.tensor_copy(picked[:], pool_scales[:].bitcast(U8).indirect(offsets[:]))
-        for quad, queue in ((1, nc.scalar), (2, nc.sync), (3, nc.scalar)):
+        for quad, queue in ((0, nc.scalar), (1, nc.sync), (3, nc.scalar)):
             queue.dma_start(
-                out=key_scales[32 * quad : 32 * quad + 4, :], in_=picked[4 * quad : 4 * quad + 4, :].bitcast(I32)
+                out=key_scales[32 * quad + 8 : 32 * quad + 12, :],
+                in_=picked[64 + 4 * quad : 68 + 4 * quad, :].bitcast(I32),
             )
-        nc.vector.tensor_copy(key_scales[0:4, :], picked[0:4, :].bitcast(I32))
+        nc.vector.tensor_copy(key_scales[64:76, :], picked[64:76, :].bitcast(I32))
         q_bf = [
             keep.tile([P, P, PACK], BF16, name="q_bf0", align_bytes=256),
             keep.tile([P, P, PACK], BF16, name="q_bf1", align_bytes=256),
@@ -79,7 +80,7 @@ def tile_attend_maxsim_kernel(tc, qT, k_words, k_scales, offs, out):
                 lhsT=q_codes[:, h * P : (h + 1) * P].bitcast(FP8X4),
                 lhsT_scale=q_scales[:, h * P : (h + 1) * P],
                 rhs=key_words[c][:, at : at + width].bitcast(FP8X4),
-                rhs_scale=key_scales[:].bitcast(U8)[:, lo : lo + width],
+                rhs_scale=key_scales[:].bitcast(U8)[8:P, lo : lo + width],
                 start=True,
                 stop=True,
             )

from contextlib import ExitStack

import concourse.mybir as mybir

N, T, DIM, NQ, SEG = 512, 2048, 512, 256, 32

F32 = mybir.dt.float32
BF16 = mybir.dt.bfloat16
I32 = mybir.dt.int32
U32 = mybir.dt.uint32
U16 = mybir.dt.uint16
U8 = mybir.dt.uint8
FP8X4 = mybir.dt.float8_e4m3fn_x4

P = 128
PACK = 4
FLOPS = 2 * NQ * N * DIM


def tile_attend_maxsim_kernel(tc, qT, k_words, k_scales, offs, out):
    nc = tc.nc
    with ExitStack() as ctx:
        keep = ctx.enter_context(tc.tile_pool(name="keep", bufs=1))
        psum = ctx.enter_context(tc.psum_pool(name="psum", bufs=1))

        offsets = keep.tile([P, N // 16], U16, name="offsets")
        pool_scales = keep.tile([P, T // 4], I32, name="pool_scales", align_bytes=256)
        pool_words = keep.tile([P, T], I32, name="pool_words", align_bytes=256)
        q_raw = keep.tile([P, PACK, NQ], F32, name="q_raw", align_bytes=256)

        key_scales = keep.tile([P, N // 4], I32, name="key_scales", align_bytes=256)
        landed = keep.tile([P, T // 4], I32, name="landed", align_bytes=256)
        nc.scalar.dma_start(out=landed[64:80, :], in_=k_scales[0].bitcast(I32))
        nc.vector.memset(pool_scales[:], 0)
        nc.vector.memset(key_scales[:], 0)
        nc.sync.dma_start(offsets[:], offs)
        nc.sync.dma_start(out=q_raw[:], in_=qT[0].rearrange("(p j) w -> p j w", j=PACK))
        nc.sync.dma_start(out=pool_words[:], in_=k_words[0].rearrange("p t r -> p (t r)").bitcast(I32))

        q_codes = keep.tile([P, NQ], U32, name="q_codes", align_bytes=256)
        q_scales = keep.tile([P, NQ], U8, name="q_scales", align_bytes=256)
        nc.vector.tensor_copy(pool_scales[64:80, :], landed[64:80, :])
        picked = keep.tile([P, N], U8, name="picked", align_bytes=256)
        nc.vector.tensor_copy(picked[:], pool_scales[:].bitcast(U8).indirect(offsets[:]))
        for quad, queue in ((0, nc.scalar), (1, nc.sync), (3, nc.scalar)):
            queue.dma_start(
                out=key_scales[32 * quad + 8 : 32 * quad + 12, :],
                in_=picked[64 + 4 * quad : 68 + 4 * quad, :].bitcast(I32),
            )
        nc.vector.tensor_copy(key_scales[64:76, :], picked[64:76, :].bitcast(I32))
        q_bf = [
            keep.tile([P, P, PACK], BF16, name="q_bf0", align_bytes=256),
            keep.tile([P, P, PACK], BF16, name="q_bf1", align_bytes=256),
        ]
        for h, cast in enumerate((nc.vector.tensor_copy, nc.vector.tensor_copy)):
            cast(
                out=q_bf[h][:].rearrange("p (u i b) j -> p u b j i", u=2, i=4),
                in_=q_raw[:, :, h:NQ:2].rearrange("p j (b u i) -> p u b j i", u=2, i=4),
            )
        for h in (1, 0):
            nc.vector.quantize_mx(
                out=q_codes[:, h * P : (h + 1) * P].bitcast(FP8X4),
                scales=q_scales[:, h * P : (h + 1) * P],
                in_=q_bf[h][:].rearrange("p w j -> p (w j)"),
            )

        key_words = []
        for c in range(N // P):
            kw = keep.tile([P, P], U32, name="key_words%d" % c, align_bytes=256)
            cols = slice(c * P // 16, (c + 1) * P // 16)
            nc.vector.tensor_copy(kw[:], pool_words[:].bitcast(U32).indirect(offsets[:, cols]))
            key_words.append(kw)

        best = keep.tile([P, 2, N // SEG], F32, name="best", align_bytes=256)
        for i, (h, lo, width) in enumerate([(h, c * P, P) for c in range(N // P) for h in (1, 0)]):
            c, at = divmod(lo, P)
            scores = psum.tile([P, width], F32, name="scores%d" % i)
            nc.tensor.matmul_mx(
                out=scores[:],
                lhsT=q_codes[:, h * P : (h + 1) * P].bitcast(FP8X4),
                lhsT_scale=q_scales[:, h * P : (h + 1) * P],
                rhs=key_words[c][:, at : at + width].bitcast(FP8X4),
                rhs_scale=key_scales[:].bitcast(U8)[8:P, lo : lo + width],
                start=True,
                stop=True,
            )
            nc.vector.tensor_reduce(
                out=best[:, h, lo // SEG : (lo + width) // SEG],
                in_=scores[:].rearrange("p (j s) -> p j s", s=SEG),
                axis=mybir.AxisListType.X,
                op=mybir.AluOpType.max,
            )
        nc.sync.dma_start(
            out=out[0].rearrange("(b a h) j -> a b (h j)", a=8, h=2), in_=best[:].rearrange("p h j -> p (h j)")
        )
